import numpy as np
import ml_dtypes


def mxq(x, axis, fmt="e4m3"):
    dtype, down = {"e4m3": (ml_dtypes.float8_e4m3fn, 7), "e5m2": (ml_dtypes.float8_e5m2, 14)}[fmt]
    v = np.moveaxis(np.asarray(x, np.float32).astype(ml_dtypes.bfloat16).astype(np.float64), axis, -1)
    blocks = v.reshape(v.shape[:-1] + (-1, 32))
    amax = np.abs(blocks).max(-1, keepdims=True)
    byte = np.maximum(np.where(amax > 0, np.frexp(amax)[1] - 1 + 127, 0) - down, 1)
    scale = np.exp2(byte - 127.0)
    codes = (blocks / scale).astype(np.float32).astype(dtype).astype(np.float64)
    return np.moveaxis((codes * scale).reshape(v.shape), -1, axis)


WIDE = False


def mx_kscale(k):
    if not WIDE:
        return np.ones(k)
    levels = np.array([10, -10, 5, -5, 0])
    if k % 512:
        return np.exp2(np.random.permutation(np.resize(levels, k // 32))).repeat(32)
    a = np.empty((k // 512, 16))
    for p in range(k // 512):
        a[p, :8] = np.random.permutation(np.resize(levels, 8))
        for g in range(8):
            far = levels[np.abs(levels - a[p, g]) >= 10]
            a[p, g + 8] = far[np.random.randint(len(far))]
    return np.exp2(a.ravel()).repeat(32)


def f64(x):
    return np.asarray(x).astype(np.float64)


def striped(idx):
    return np.tile(idx.reshape(-1, 16).T, (8, 1)).astype(np.uint16)


def unstriped(offs):
    return offs[:16].T.reshape(-1).astype(np.int64)


def pack_weight(w):
    k, n = w.shape
    w = f64(np.asarray(w, np.float32).astype(ml_dtypes.bfloat16)).reshape(k // 32, 32, n)
    amax = np.abs(w).max(1)
    byte = np.clip(np.where(amax > 0, np.frexp(amax)[1] - 1 + 127 - 7, 1), 1, 254)
    scaled = (w * np.exp2(127.0 - byte)[:, None, :]).reshape(k, n).astype(np.float32)
    words = np.ascontiguousarray(scaled.reshape(k // 512, 128, 4, n).transpose(0, 1, 3, 2)).astype(ml_dtypes.float8_e4m3fn).view(np.uint8)
    return words, np.ascontiguousarray(byte.astype(np.uint8).reshape(k // 512, 16, n))


def unpack_weight(words, scales):
    g, p, n, _ = words.shape
    vals = np.ascontiguousarray(words).view(ml_dtypes.float8_e4m3fn).astype(np.float64) * np.repeat(np.exp2(scales.astype(np.float64) - 127.0), 8, axis=1)[..., None]
    return vals.transpose(0, 1, 3, 2).reshape(g * 512, n)


def planes(y):
    n, m = y.shape
    v = y.astype(np.float32).astype(ml_dtypes.bfloat16).astype(np.float64).reshape(n // 32, 32, m)
    top = np.abs(v).max(1)
    byte = np.clip(np.where(top > 0, np.frexp(top)[1] - 1 + 127 - 7, 1), 1, 254)
    codes = (v * np.exp2(127.0 - byte)[:, None, :]).reshape(n, m).astype(np.float32).astype(ml_dtypes.float8_e4m3fn).view(np.uint8)
    words = codes.reshape(n // 512, 128, 4, m).transpose(0, 1, 3, 2)
    return np.ascontiguousarray(words), np.ascontiguousarray(byte.astype(np.uint8).reshape(n // 512, 16, m))


K, T, S, N = 1024, 2048, 512, 512


def setup_inputs():
    n = np.random.standard_normal
    s = mx_kscale(K)[:, None]
    packed_xT = pack_weight(n((K, T)) * s)
    return {
        "x_words": packed_xT[0],
        "x_scales": packed_xT[1],
        "eT": (n((K, S)) * s).astype(np.float32),
        "w1": (n((K, N)) / np.sqrt(2 * K) / s).astype(np.float32),
        "w2": (n((K, N)) / np.sqrt(2 * K) / s).astype(np.float32),
        "w3": (n((K, N)) / np.sqrt(2 * K) / s).astype(np.float32),
        "w4": (n((K, N)) / np.sqrt(2 * K) / s).astype(np.float32),
        "dec": (n((N, S))).astype(np.float32),
        "offs": striped(np.random.permutation(T)[:S]),
    }


def reference(x_words, x_scales, eT, w1, w2, w3, w4, dec, offs):
    eTq = mxq(f64(eT), 0, "e4m3")
    xq = unpack_weight(x_words, x_scales)[:, unstriped(offs)]
    g = mxq(f64(w1), 0, "e4m3").T @ eTq + mxq(f64(w2), 0, "e4m3").T @ xq
    h = mxq(f64(w3), 0, "e4m3").T @ eTq + mxq(f64(w4), 0, "e4m3").T @ xq
    out_0 = f64(dec) * g + h + f64(dec)
    return (out_0,) + planes(out_0)

@@ -1,0 +1,182 @@
+from contextlib import ExitStack
+
+import concourse.mybir as mybir
+
+K, T, S, N = 1024, 2048, 512, 512
+FLOPS = 2 * 4 * K * S * N
+
+F32 = mybir.dt.float32
+BF16 = mybir.dt.bfloat16
+I32 = mybir.dt.int32
+U32 = mybir.dt.uint32
+U16 = mybir.dt.uint16
+U8 = mybir.dt.uint8
+FP8X4 = mybir.dt.float8_e4m3fn_x4
+ADD = mybir.AluOpType.add
+MULT = mybir.AluOpType.mult
+
+P = 128
+PACK = 4
+K_PASS = P * PACK
+PASSES = K // K_PASS
+HALF = S // 2
+SCALAR_COLS = 320
+SCALAR_COLS_LAST = 160
+
+
+def tile_picked_zcft_add_po_kernel(tc, x_words, x_scales, eT, w1, w2, w3, w4, dec, offs, out_0, out_1, out_2):
+    nc = tc.nc
+    with ExitStack() as ctx:
+        keep = ctx.enter_context(tc.tile_pool(name="keep", bufs=1))
+        psum = ctx.enter_context(tc.psum_pool(name="psum", bufs=1))
+
+        def load_rows(src, name):
+            raw = keep.tile([P, PACK, src.shape[1]], F32, name=name, align_bytes=64)
+            nc.sync.dma_start(out=raw[:], in_=src.rearrange("(p j) c -> p j c", j=PACK))
+            return raw
+
+        def rows_of(src, o):
+            return src[o * K_PASS : (o + 1) * K_PASS, :]
+
+        def load_words(o):
+            words = keep.tile([P, T], U32, name=f"x_table{o}", align_bytes=64)
+            nc.sync.dma_start(out=words[:].bitcast(I32), in_=x_words[o].rearrange("p c r -> p (c r)").bitcast(I32))
+            return words
+
+        scale_table = keep.tile([P, T], U8, name="scale_table", align_bytes=64)
+        nc.vector.memset(scale_table[:].bitcast(I32), 0)
+        for q in range(4):
+            nc.gpsimd.dma_start(
+                out=scale_table[32 * q : 32 * q + 4 * PASSES, :].bitcast(I32),
+                in_=x_scales[:, 4 * q : 4 * q + 4, :].bitcast(I32),
+            )
+
+        raw = {}
+        raw["e", 0] = load_rows(rows_of(eT, 0), "e_raw0")
+        offsets = keep.tile([P, S // 16], U16, name="offsets")
+        nc.sync.dma_start(offsets[:], offs)
+        raw["w1", 0] = load_rows(rows_of(w1, 0), "w1_raw0")
+        table = {0: load_words(0)}
+        raw["w2", 0] = load_rows(rows_of(w2, 0), "w2_raw0")
+        raw["e", 1] = load_rows(rows_of(eT, 1), "e_raw1")
+        raw["w1", 1] = load_rows(rows_of(w1, 1), "w1_raw1")
+        table[1] = load_words(1)
+        raw["w2", 1] = load_rows(rows_of(w2, 1), "w2_raw1")
+        dec_sb = load_rows(dec, "dec_sb")
+        raw["w3", 0] = load_rows(rows_of(w3, 0), "w3_raw0")
+        raw["w3", 1] = load_rows(rows_of(w3, 1), "w3_raw1")
+        raw["w4", 0] = load_rows(rows_of(w4, 0), "w4_raw0")
+        raw["w4", 1] = load_rows(rows_of(w4, 1), "w4_raw1")
+
+        def split_copy(dst, src, cut):
+            nc.scalar.copy(out=dst[:, :cut], in_=src[:, :cut])
+            nc.vector.tensor_copy(out=dst[:, cut:], in_=src[:, cut:])
+
+        def round_moving(src, name, scalar_cols):
+            width = src.shape[2]
+            grouped = keep.tile([P, width, PACK], BF16, name=name, align_bytes=64)
+            split_copy(
+                grouped[:].rearrange("p (c i) j -> p c j i", i=4),
+                src[:].rearrange("p j (c i) -> p c j i", i=4),
+                scalar_cols // 4,
+            )
+            return grouped[:].rearrange("p c j -> p (c j)")
+
+        def round_weights(src, name, scalar_cols):
+            grouped = keep.tile([P, PACK, P, PACK], BF16, name=name, align_bytes=64)
+            split_copy(
+                grouped[:].rearrange("p t m j -> p m j t"),
+                src[:].rearrange("p j (m t) -> p m j t", t=PACK),
+                scalar_cols // PACK,
+            )
+            return grouped[:].rearrange("p t m j -> p (t m j)")
+
+        def quantize(grouped, name, pieces):
+            codes = keep.tile([P, 512], U32, name=name + "_codes", align_bytes=64)
+            scales = keep.tile([P, 512], U8, name=name + "_scales", align_bytes=64)
+            step = 512 // pieces
+            for c in range(0, 512, step):
+                nc.vector.quantize_mx(
+                    out=codes[:, c : c + step].bitcast(FP8X4),
+                    scales=scales[:, c : c + step],
+                    in_=grouped[:, PACK * c : PACK * (c + step)],
+                )
+            return codes, scales
+
+        def gather_words(o):
+            picked = keep.tile([P, S], U32, name=f"x_picked{o}", align_bytes=64)
+            nc.vector.tensor_copy(picked[:], table[o][:].indirect(offsets[:]))
+            return picked
+
+        def multiply(banks, weights, moving, start, stop):
+            codes, scales = weights
+            for t in range(PACK):
+                cols = slice(t * P, (t + 1) * P)
+                nc.tensor.matmul_mx(
+                    out=banks[t][:],
+                    lhsT=codes[:, cols].bitcast(FP8X4),
+                    lhsT_scale=scales[:, cols],
+                    rhs=moving[0].bitcast(FP8X4),
+                    rhs_scale=moving[1],
+                    start=start,
+                    stop=stop,
+                )
+
+        def weights(name, o, last=False):
+            grouped = round_weights(raw[name, o], f"{name}_bf{o}", SCALAR_COLS_LAST if last else SCALAR_COLS)
+            return quantize(grouped, f"{name}_{o}", PACK if last else 1)
+
+        g_banks = [psum.tile([P, S], F32, name=f"g{t}") for t in range(PACK)]
+        h_banks = [psum.tile([P, S], F32, name=f"h{t}") for t in range(PACK)]
+
+        picked_scales = keep.tile([P, S], U8, name="picked_scales", align_bytes=64)
+        e_q, x_q = {}, {}
+        for o in range(PASSES):
+            codes, scales = quantize(round_moving(raw["e", o], f"e_bf{o}", SCALAR_COLS), f"e_{o}", 1)
+            e_q[o] = (codes[:], scales[:])
+            multiply(g_banks, weights("w1", o), e_q[o], o == 0, False)
+            if o == 0:
+                nc.vector.tensor_copy(picked_scales[:], scale_table[:].indirect(offsets[:]))
+            x_q[o] = (gather_words(o)[:], picked_scales[4 * o :, :])
+            multiply(g_banks, weights("w2", o), x_q[o], False, o == PASSES - 1)
+
+        scaled = keep.tile([P, PACK, S], F32, name="scaled")
+        for t in range(PACK):
+            nc.vector.scalar_tensor_tensor(
+                out=scaled[:, t, :], in0=g_banks[t][:], scalar=1.0, in1=dec_sb[:, t, :], op0=ADD, op1=MULT
+            )
+
+        for o in range(PASSES):
+            multiply(h_banks, weights("w3", o), e_q[o], o == 0, False)
+        for o in range(PASSES):
+            multiply(h_banks, weights("w4", o, last=(o == PASSES - 1)), x_q[o], False, o == PASSES - 1)
+
+        y_codes = keep.tile([P, S], U32, name="y_codes", align_bytes=64)
+        y_scales = keep.tile([P, S], U8, name="y_scales", align_bytes=64)
+        out_rows = out_0.rearrange("(p t) j -> p t j", t=PACK)
+        out_words = out_1[0].rearrange("p c r -> p (c r)").bitcast(I32)
+        y_bf = {}
+        for half in range(2):
+            cols = slice(half * HALF, (half + 1) * HALF)
+            y = keep.tile([P, PACK, HALF], F32, name=f"y{half}", align_bytes=64)
+            for t in range(PACK):
+                nc.vector.tensor_tensor(out=y[:, t, :], in0=h_banks[t][:, cols], in1=scaled[:, t, cols], op=ADD)
+            nc.sync.dma_start(out=out_rows[:, :, cols], in_=y[:])
+            if half == 0:
+                grouped = keep.tile([P, HALF, PACK], BF16, name="y_bf0", align_bytes=64)
+                nc.scalar.copy(
+                    out=grouped[:].rearrange("p (c i) j -> p c j i", i=4),
+                    in_=y[:].rearrange("p j (c i) -> p c j i", i=4),
+                )
+                y_bf[0] = grouped[:].rearrange("p c j -> p (c j)")
+            else:
+                y_bf[1] = round_moving(y, "y_bf1", 96)
+        for half in range(2):
+            cols = slice(half * HALF, (half + 1) * HALF)
+            nc.vector.quantize_mx(out=y_codes[:, cols].bitcast(FP8X4), scales=y_scales[:, cols], in_=y_bf[half])
+            nc.sync.dma_start(out=out_words[:, cols], in_=y_codes[:, cols].bitcast(I32))
+        for q in range(4):
+            queue = nc.scalar if q % 2 else nc.sync
+            queue.dma_start(
+                out=out_2[0, 4 * q : 4 * q + 4, :].bitcast(I32), in_=y_scales[32 * q : 32 * q + 4, :].bitcast(I32)
+            )

@@ -20,8 +20,10 @@ PACK = 4
 K_PASS = P * PACK
 PASSES = K // K_PASS
 HALF = S // 2
-SCALAR_COLS = 320
-SCALAR_COLS_LAST = 160
+SCALAR_COLS = 224
+SCALAR_COLS_W3 = (448, 320)
+SCALAR_COLS_PAIR = (256, 128)
+SCALAR_COLS_OUT = 80
 
 
 def tile_picked_zcft_add_po_kernel(tc, x_words, x_scales, eT, w1, w2, w3, w4, dec, offs, out_0, out_1, out_2):
@@ -51,12 +53,13 @@ def tile_picked_zcft_add_po_kernel(tc, x_words, x_scales, eT, w1, w2, w3, w4, de
                 in_=x_scales[:, 4 * q : 4 * q + 4, :].bitcast(I32),
             )
 
+
         raw = {}
         raw["e", 0] = load_rows(rows_of(eT, 0), "e_raw0")
-        offsets = keep.tile([P, S // 16], U16, name="offsets")
-        nc.sync.dma_start(offsets[:], offs)
         raw["w1", 0] = load_rows(rows_of(w1, 0), "w1_raw0")
         table = {0: load_words(0)}
+        offsets = keep.tile([P, S // 16], U16, name="offsets")
+        nc.sync.dma_start(offsets[:], offs)
         raw["w2", 0] = load_rows(rows_of(w2, 0), "w2_raw0")
         raw["e", 1] = load_rows(rows_of(eT, 1), "e_raw1")
         raw["w1", 1] = load_rows(rows_of(w1, 1), "w1_raw1")
@@ -66,7 +69,12 @@ def tile_picked_zcft_add_po_kernel(tc, x_words, x_scales, eT, w1, w2, w3, w4, de
         raw["w3", 0] = load_rows(rows_of(w3, 0), "w3_raw0")
         raw["w3", 1] = load_rows(rows_of(w3, 1), "w3_raw1")
         raw["w4", 0] = load_rows(rows_of(w4, 0), "w4_raw0")
-        raw["w4", 1] = load_rows(rows_of(w4, 1), "w4_raw1")
+        last_rows = rows_of(w4, 1).rearrange("(p j) c -> p j c", j=PACK)
+        last_pairs = []
+        for u in range(2):
+            pair = keep.tile([P, 2, N], F32, name=f"w4_pair{u}", align_bytes=64)
+            nc.sync.dma_start(out=pair[:], in_=last_rows[:, 2 * u : 2 * u + 2, :])
+            last_pairs.append(pair)
 
         def split_copy(dst, src, cut):
             nc.scalar.copy(out=dst[:, :cut], in_=src[:, :cut])
@@ -110,24 +118,34 @@ def tile_picked_zcft_add_po_kernel(tc, x_words, x_scales, eT, w1, w2, w3, w4, de
 
         def multiply(banks, weights, moving, start, stop):
             codes, scales = weights
-            for t in range(PACK):
+            for (t, first, width), bank in banks.items():
+                positions = slice(first, first + width)
                 cols = slice(t * P, (t + 1) * P)
                 nc.tensor.matmul_mx(
-                    out=banks[t][:],
+                    out=bank[:],
                     lhsT=codes[:, cols].bitcast(FP8X4),
                     lhsT_scale=scales[:, cols],
-                    rhs=moving[0].bitcast(FP8X4),
-                    rhs_scale=moving[1],
+                    rhs=moving[0][:, positions].bitcast(FP8X4),
+                    rhs_scale=moving[1][:, positions],
                     start=start,
                     stop=stop,
                 )
 
-        def weights(name, o, last=False):
-            grouped = round_weights(raw[name, o], f"{name}_bf{o}", SCALAR_COLS_LAST if last else SCALAR_COLS)
-            return quantize(grouped, f"{name}_{o}", PACK if last else 1)
+        def weights(name, o, scalar_cols=SCALAR_COLS):
+            grouped = round_weights(raw[name, o], f"{name}_bf{o}", scalar_cols)
+            return quantize(grouped, f"{name}_{o}", 1)
 
-        g_banks = [psum.tile([P, S], F32, name=f"g{t}") for t in range(PACK)]
-        h_banks = [psum.tile([P, S], F32, name=f"h{t}") for t in range(PACK)]
+        def last_weights():
+            grouped = keep.tile([P, PACK, P, PACK], BF16, name="last_bf", align_bytes=64)
+            for u in range(2):
+                split_copy(
+                    grouped[:, :, :, 2 * u : 2 * u + 2].rearrange("p t m j -> p m j t"),
+                    last_pairs[u][:].rearrange("p j (m t) -> p m j t", t=PACK),
+                    SCALAR_COLS_PAIR[u] // PACK,
+                )
+            return quantize(grouped[:].rearrange("p t m j -> p (t m j)"), "last", PACK)
+
+        g_banks = {(t, 0, S): psum.tile([P, S], F32, name=f"g{t}", tag=f"reused{t}") for t in range(PACK)}
 
         picked_scales = keep.tile([P, S], U8, name="picked_scales", align_bytes=64)
         e_q, x_q = {}, {}
@@ -143,37 +161,47 @@ def tile_picked_zcft_add_po_kernel(tc, x_words, x_scales, eT, w1, w2, w3, w4, de
         scaled = keep.tile([P, PACK, S], F32, name="scaled")
         for t in range(PACK):
             nc.vector.scalar_tensor_tensor(
-                out=scaled[:, t, :], in0=g_banks[t][:], scalar=1.0, in1=dec_sb[:, t, :], op0=ADD, op1=MULT
+                out=scaled[:, t, :], in0=g_banks[t, 0, S][:], scalar=1.0, in1=dec_sb[:, t, :], op0=ADD, op1=MULT
             )
 
+        h_banks = {}
+        for half in range(2):
+            for t in range(PACK):
+                tag = f"reused{t}" if half else f"fresh{t}"
+                h_banks[t, half * HALF, HALF] = psum.tile([P, HALF], F32, name=f"h{t}_{half}", tag=tag)
         for o in range(PASSES):
-            multiply(h_banks, weights("w3", o), e_q[o], o == 0, False)
-        for o in range(PASSES):
-            multiply(h_banks, weights("w4", o, last=(o == PASSES - 1)), x_q[o], False, o == PASSES - 1)
+            multiply(h_banks, weights("w3", o, SCALAR_COLS_W3[o]), e_q[o], o == 0, False)
+        multiply(h_banks, weights("w4", 0), x_q[0], False, False)
+        multiply(h_banks, last_weights(), x_q[1], False, True)
 
         y_codes = keep.tile([P, S], U32, name="y_codes", align_bytes=64)
         y_scales = keep.tile([P, S], U8, name="y_scales", align_bytes=64)
         out_rows = out_0.rearrange("(p t) j -> p t j", t=PACK)
         out_words = out_1[0].rearrange("p c r -> p (c r)").bitcast(I32)
-        y_bf = {}
-        for half in range(2):
-            cols = slice(half * HALF, (half + 1) * HALF)
+        halves = [slice(0, HALF), slice(HALF, S)]
+        y_bf = []
+        for half, cols in enumerate(halves):
             y = keep.tile([P, PACK, HALF], F32, name=f"y{half}", align_bytes=64)
             for t in range(PACK):
-                nc.vector.tensor_tensor(out=y[:, t, :], in0=h_banks[t][:, cols], in1=scaled[:, t, cols], op=ADD)
-            nc.sync.dma_start(out=out_rows[:, :, cols], in_=y[:])
-            if half == 0:
-                grouped = keep.tile([P, HALF, PACK], BF16, name="y_bf0", align_bytes=64)
-                nc.scalar.copy(
-                    out=grouped[:].rearrange("p (c i) j -> p c j i", i=4),
-                    in_=y[:].rearrange("p j (c i) -> p c j i", i=4),
+                nc.vector.tensor_tensor(
+                    out=y[:, t, :], in0=h_banks[t, half * HALF, HALF][:], in1=scaled[:, t, cols], op=ADD
                 )
-                y_bf[0] = grouped[:].rearrange("p c j -> p (c j)")
+                if t % 2:
+                    nc.sync.dma_start(out=out_rows[:, t - 1 : t + 1, cols], in_=y[:, t - 1 : t + 1, :])
+            rounded = keep.tile([P, HALF, PACK], BF16, name=f"y_bf{half}", align_bytes=64)
+            dst = rounded[:].rearrange("p (c i) j -> p c j i", i=4)
+            src = y[:].rearrange("p j (c i) -> p c j i", i=4)
+            if half == 0:
+                nc.scalar.copy(out=dst, in_=src)
             else:
-                y_bf[1] = round_moving(y, "y_bf1", 96)
-        for half in range(2):
-            cols = slice(half * HALF, (half + 1) * HALF)
-            nc.vector.quantize_mx(out=y_codes[:, cols].bitcast(FP8X4), scales=y_scales[:, cols], in_=y_bf[half])
+                split_copy(dst, src, SCALAR_COLS_OUT // 4)
+            y_bf.append(rounded)
+        for half, cols in enumerate(halves):
+            nc.vector.quantize_mx(
+                out=y_codes[:, cols].bitcast(FP8X4),
+                scales=y_scales[:, cols],
+                in_=y_bf[half][:].rearrange("p c j -> p (c j)"),
+            )
             nc.sync.dma_start(out=out_words[:, cols], in_=y_codes[:, cols].bitcast(I32))
         for q in range(4):
             queue = nc.scalar if q % 2 else nc.sync

@@ -20,9 +20,10 @@ PACK = 4
 K_PASS = P * PACK
 PASSES = K // K_PASS
 HALF = S // 2
-SCALAR_COLS = 224
+SCALAR_COLS = 288
 SCALAR_COLS_W3 = (448, 320)
-SCALAR_COLS_PAIR = (256, 128)
+SCALAR_COLS_W4 = 224
+SCALAR_COLS_PAIR = (256, 160)
 SCALAR_COLS_OUT = 80
 
 
@@ -80,6 +81,16 @@ def tile_picked_zcft_add_po_kernel(tc, x_words, x_scales, eT, w1, w2, w3, w4, de
             nc.scalar.copy(out=dst[:, :cut], in_=src[:, :cut])
             nc.vector.tensor_copy(out=dst[:, cut:], in_=src[:, cut:])
 
+        def deal_copy(dst, src, cut):
+            nc.scalar.copy(
+                out=dst.rearrange("p t m j -> p m j t")[:, :cut],
+                in_=src.rearrange("p j (m t) -> p m j t", t=PACK)[:, :cut],
+            )
+            nc.vector.tensor_copy(
+                out=dst.rearrange("p t m j -> p m t j")[:, cut:],
+                in_=src.rearrange("p j (m t) -> p m t j", t=PACK)[:, cut:],
+            )
+
         def round_moving(src, name, scalar_cols):
             width = src.shape[2]
             grouped = keep.tile([P, width, PACK], BF16, name=name, align_bytes=64)
@@ -92,11 +103,7 @@ def tile_picked_zcft_add_po_kernel(tc, x_words, x_scales, eT, w1, w2, w3, w4, de
 
         def round_weights(src, name, scalar_cols):
             grouped = keep.tile([P, PACK, P, PACK], BF16, name=name, align_bytes=64)
-            split_copy(
-                grouped[:].rearrange("p t m j -> p m j t"),
-                src[:].rearrange("p j (m t) -> p m j t", t=PACK),
-                scalar_cols // PACK,
-            )
+            deal_copy(grouped[:], src[:], scalar_cols // PACK)
             return grouped[:].rearrange("p t m j -> p (t m j)")
 
         def quantize(grouped, name, pieces):
@@ -138,11 +145,7 @@ def tile_picked_zcft_add_po_kernel(tc, x_words, x_scales, eT, w1, w2, w3, w4, de
         def last_weights():
             grouped = keep.tile([P, PACK, P, PACK], BF16, name="last_bf", align_bytes=64)
             for u in range(2):
-                split_copy(
-                    grouped[:, :, :, 2 * u : 2 * u + 2].rearrange("p t m j -> p m j t"),
-                    last_pairs[u][:].rearrange("p j (m t) -> p m j t", t=PACK),
-                    SCALAR_COLS_PAIR[u] // PACK,
-                )
+                deal_copy(grouped[:, :, :, 2 * u : 2 * u + 2], last_pairs[u][:], SCALAR_COLS_PAIR[u] // PACK)
             return quantize(grouped[:].rearrange("p t m j -> p (t m j)"), "last", PACK)
 
         g_banks = {(t, 0, S): psum.tile([P, S], F32, name=f"g{t}", tag=f"reused{t}") for t in range(PACK)}
@@ -171,7 +174,7 @@ def tile_picked_zcft_add_po_kernel(tc, x_words, x_scales, eT, w1, w2, w3, w4, de
                 h_banks[t, half * HALF, HALF] = psum.tile([P, HALF], F32, name=f"h{t}_{half}", tag=tag)
         for o in range(PASSES):
             multiply(h_banks, weights("w3", o, SCALAR_COLS_W3[o]), e_q[o], o == 0, False)
-        multiply(h_banks, weights("w4", 0), x_q[0], False, False)
+        multiply(h_banks, weights("w4", 0, SCALAR_COLS_W4), x_q[0], False, False)
         multiply(h_banks, last_weights(), x_q[1], False, True)
 
         y_codes = keep.tile([P, S], U32, name="y_codes", align_bytes=64)

from contextlib import ExitStack

import concourse.mybir as mybir

K, T, S, N = 1024, 2048, 512, 512
FLOPS = 2 * 4 * K * S * N

F32 = mybir.dt.float32
BF16 = mybir.dt.bfloat16
I32 = mybir.dt.int32
U32 = mybir.dt.uint32
U16 = mybir.dt.uint16
U8 = mybir.dt.uint8
FP8X4 = mybir.dt.float8_e4m3fn_x4
ADD = mybir.AluOpType.add
MULT = mybir.AluOpType.mult

P = 128
PACK = 4
K_PASS = P * PACK
PASSES = K // K_PASS
HALF = S // 2
SCALAR_COLS = 288
SCALAR_COLS_W3 = (448, 320)
SCALAR_COLS_W4 = 224
SCALAR_COLS_PAIR = (256, 160)
SCALAR_COLS_OUT = 80


def tile_picked_zcft_add_po_kernel(tc, x_words, x_scales, eT, w1, w2, w3, w4, dec, offs, out_0, out_1, out_2):
    nc = tc.nc
    with ExitStack() as ctx:
        keep = ctx.enter_context(tc.tile_pool(name="keep", bufs=1))
        psum = ctx.enter_context(tc.psum_pool(name="psum", bufs=1))

        def load_rows(src, name):
            raw = keep.tile([P, PACK, src.shape[1]], F32, name=name, align_bytes=64)
            nc.sync.dma_start(out=raw[:], in_=src.rearrange("(p j) c -> p j c", j=PACK))
            return raw

        def rows_of(src, o):
            return src[o * K_PASS : (o + 1) * K_PASS, :]

        def load_words(o):
            words = keep.tile([P, T], U32, name=f"x_table{o}", align_bytes=64)
            nc.sync.dma_start(out=words[:].bitcast(I32), in_=x_words[o].rearrange("p c r -> p (c r)").bitcast(I32))
            return words

        scale_table = keep.tile([P, T], U8, name="scale_table", align_bytes=64)
        nc.vector.memset(scale_table[:].bitcast(I32), 0)
        for q in range(4):
            nc.gpsimd.dma_start(
                out=scale_table[32 * q : 32 * q + 4 * PASSES, :].bitcast(I32),
                in_=x_scales[:, 4 * q : 4 * q + 4, :].bitcast(I32),
            )


        raw = {}
        raw["e", 0] = load_rows(rows_of(eT, 0), "e_raw0")
        raw["w1", 0] = load_rows(rows_of(w1, 0), "w1_raw0")
        table = {0: load_words(0)}
        offsets = keep.tile([P, S // 16], U16, name="offsets")
        nc.sync.dma_start(offsets[:], offs)
        raw["w2", 0] = load_rows(rows_of(w2, 0), "w2_raw0")
        raw["e", 1] = load_rows(rows_of(eT, 1), "e_raw1")
        raw["w1", 1] = load_rows(rows_of(w1, 1), "w1_raw1")
        table[1] = load_words(1)
        raw["w2", 1] = load_rows(rows_of(w2, 1), "w2_raw1")
        dec_sb = load_rows(dec, "dec_sb")
        raw["w3", 0] = load_rows(rows_of(w3, 0), "w3_raw0")
        raw["w3", 1] = load_rows(rows_of(w3, 1), "w3_raw1")
        raw["w4", 0] = load_rows(rows_of(w4, 0), "w4_raw0")
        last_rows = rows_of(w4, 1).rearrange("(p j) c -> p j c", j=PACK)
        last_pairs = []
        for u in range(2):
            pair = keep.tile([P, 2, N], F32, name=f"w4_pair{u}", align_bytes=64)
            nc.sync.dma_start(out=pair[:], in_=last_rows[:, 2 * u : 2 * u + 2, :])
            last_pairs.append(pair)

        def split_copy(dst, src, cut):
            nc.scalar.copy(out=dst[:, :cut], in_=src[:, :cut])
            nc.vector.tensor_copy(out=dst[:, cut:], in_=src[:, cut:])

        def deal_copy(dst, src, cut):
            nc.scalar.copy(
                out=dst.rearrange("p t m j -> p m j t")[:, :cut],
                in_=src.rearrange("p j (m t) -> p m j t", t=PACK)[:, :cut],
            )
            nc.vector.tensor_copy(
                out=dst.rearrange("p t m j -> p m t j")[:, cut:],
                in_=src.rearrange("p j (m t) -> p m t j", t=PACK)[:, cut:],
            )

        def round_moving(src, name, scalar_cols):
            width = src.shape[2]
            grouped = keep.tile([P, width, PACK], BF16, name=name, align_bytes=64)
            split_copy(
                grouped[:].rearrange("p (c i) j -> p c j i", i=4),
                src[:].rearrange("p j (c i) -> p c j i", i=4),
                scalar_cols // 4,
            )
            return grouped[:].rearrange("p c j -> p (c j)")

        def round_weights(src, name, scalar_cols):
            grouped = keep.tile([P, PACK, P, PACK], BF16, name=name, align_bytes=64)
            deal_copy(grouped[:], src[:], scalar_cols // PACK)
            return grouped[:].rearrange("p t m j -> p (t m j)")

        def quantize(grouped, name, pieces):
            codes = keep.tile([P, 512], U32, name=name + "_codes", align_bytes=64)
            scales = keep.tile([P, 512], U8, name=name + "_scales", align_bytes=64)
            step = 512 // pieces
            for c in range(0, 512, step):
                nc.vector.quantize_mx(
                    out=codes[:, c : c + step].bitcast(FP8X4),
                    scales=scales[:, c : c + step],
                    in_=grouped[:, PACK * c : PACK * (c + step)],
                )
            return codes, scales

        def gather_words(o):
            picked = keep.tile([P, S], U32, name=f"x_picked{o}", align_bytes=64)
            nc.vector.tensor_copy(picked[:], table[o][:].indirect(offsets[:]))
            return picked

        def multiply(banks, weights, moving, start, stop):
            codes, scales = weights
            for (t, first, width), bank in banks.items():
                positions = slice(first, first + width)
                cols = slice(t * P, (t + 1) * P)
                nc.tensor.matmul_mx(
                    out=bank[:],
                    lhsT=codes[:, cols].bitcast(FP8X4),
                    lhsT_scale=scales[:, cols],
                    rhs=moving[0][:, positions].bitcast(FP8X4),
                    rhs_scale=moving[1][:, positions],
                    start=start,
                    stop=stop,
                )

        def weights(name, o, scalar_cols=SCALAR_COLS):
            grouped = round_weights(raw[name, o], f"{name}_bf{o}", scalar_cols)
            return quantize(grouped, f"{name}_{o}", 1)

        def last_weights():
            grouped = keep.tile([P, PACK, P, PACK], BF16, name="last_bf", align_bytes=64)
            for u in range(2):
                deal_copy(grouped[:, :, :, 2 * u : 2 * u + 2], last_pairs[u][:], SCALAR_COLS_PAIR[u] // PACK)
            return quantize(grouped[:].rearrange("p t m j -> p (t m j)"), "last", PACK)

        g_banks = {(t, 0, S): psum.tile([P, S], F32, name=f"g{t}", tag=f"reused{t}") for t in range(PACK)}

        picked_scales = keep.tile([P, S], U8, name="picked_scales", align_bytes=64)
        e_q, x_q = {}, {}
        for o in range(PASSES):
            codes, scales = quantize(round_moving(raw["e", o], f"e_bf{o}", SCALAR_COLS), f"e_{o}", 1)
            e_q[o] = (codes[:], scales[:])
            multiply(g_banks, weights("w1", o), e_q[o], o == 0, False)
            if o == 0:
                nc.vector.tensor_copy(picked_scales[:], scale_table[:].indirect(offsets[:]))
            x_q[o] = (gather_words(o)[:], picked_scales[4 * o :, :])
            multiply(g_banks, weights("w2", o), x_q[o], False, o == PASSES - 1)

        scaled = keep.tile([P, PACK, S], F32, name="scaled")
        for t in range(PACK):
            nc.vector.scalar_tensor_tensor(
                out=scaled[:, t, :], in0=g_banks[t, 0, S][:], scalar=1.0, in1=dec_sb[:, t, :], op0=ADD, op1=MULT
            )

        h_banks = {}
        for half in range(2):
            for t in range(PACK):
                tag = f"reused{t}" if half else f"fresh{t}"
                h_banks[t, half * HALF, HALF] = psum.tile([P, HALF], F32, name=f"h{t}_{half}", tag=tag)
        for o in range(PASSES):
            multiply(h_banks, weights("w3", o, SCALAR_COLS_W3[o]), e_q[o], o == 0, False)
        multiply(h_banks, weights("w4", 0, SCALAR_COLS_W4), x_q[0], False, False)
        multiply(h_banks, last_weights(), x_q[1], False, True)

        y_codes = keep.tile([P, S], U32, name="y_codes", align_bytes=64)
        y_scales = keep.tile([P, S], U8, name="y_scales", align_bytes=64)
        out_rows = out_0.rearrange("(p t) j -> p t j", t=PACK)
        out_words = out_1[0].rearrange("p c r -> p (c r)").bitcast(I32)
        halves = [slice(0, HALF), slice(HALF, S)]
        y_bf = []
        for half, cols in enumerate(halves):
            y = keep.tile([P, PACK, HALF], F32, name=f"y{half}", align_bytes=64)
            for t in range(PACK):
                nc.vector.tensor_tensor(
                    out=y[:, t, :], in0=h_banks[t, half * HALF, HALF][:], in1=scaled[:, t, cols], op=ADD
                )
                if t % 2:
                    nc.sync.dma_start(out=out_rows[:, t - 1 : t + 1, cols], in_=y[:, t - 1 : t + 1, :])
            rounded = keep.tile([P, HALF, PACK], BF16, name=f"y_bf{half}", align_bytes=64)
            dst = rounded[:].rearrange("p (c i) j -> p c j i", i=4)
            src = y[:].rearrange("p j (c i) -> p c j i", i=4)
            if half == 0:
                nc.scalar.copy(out=dst, in_=src)
            else:
                split_copy(dst, src, SCALAR_COLS_OUT // 4)
            y_bf.append(rounded)
        for half, cols in enumerate(halves):
            nc.vector.quantize_mx(
                out=y_codes[:, cols].bitcast(FP8X4),
                scales=y_scales[:, cols],
                in_=y_bf[half][:].rearrange("p c j -> p (c j)"),
            )
            nc.sync.dma_start(out=out_words[:, cols], in_=y_codes[:, cols].bitcast(I32))
        for q in range(4):
            queue = nc.scalar if q % 2 else nc.sync
            queue.dma_start(
                out=out_2[0, 4 * q : 4 * q + 4, :].bitcast(I32), in_=y_scales[32 * q : 32 * q + 4, :].bitcast(I32)
            )
